import numpy as np
import ml_dtypes

BF16 = ml_dtypes.bfloat16


def bf(x):
    return np.asarray(x, np.float32).astype(BF16)


def f32(x):
    return np.asarray(x, np.float32)


def f64(x):
    return np.asarray(x).astype(np.float64)


def striped(idx):
    return np.tile(idx.reshape(-1, 16).T, (8, 1))


S, K, M, N, D, V = 512, 128, 512, 192, 4, 48


def setup_inputs():
    return {"table": bf(np.random.standard_normal((K, S))), "w": bf(np.random.standard_normal((K, M)) / np.sqrt(K)), "b": f32(0.5 * np.random.standard_normal((M, 1))), "offs": striped(np.random.permutation(np.tile(np.arange(S), 2))[:N])}


def reference(table, w, b, offs):
    idx = offs[:16].T.reshape(-1)
    x = f64(table)[:, idx]
    y = f64(w).T @ x
    z = y + f64(b)
    return z.reshape(M, V, D).max(axis=2)

@@ -1,0 +1,50 @@
+import concourse.mybir as mybir
+
+BF16, F32, U16 = mybir.dt.bfloat16, mybir.dt.float32, mybir.dt.uint16
+
+P = 128
+S = 512
+M = 512
+N = 192
+GROUP = 4
+V = N // GROUP
+BLOCKS = M // P
+
+FLOPS = 2 * P * M * N
+
+
+def tile_gather_matmul_kernel(tc, table, w, b, offs, out):
+    nc = tc.nc
+    with (
+        tc.tile_pool(name="held", bufs=1) as held,
+        tc.psum_pool(name="psum", bufs=1) as psum,
+    ):
+        offsets = held.tile([P, N // 16], U16, name="offsets")
+        nodes = held.tile([P, S], BF16, name="nodes")
+        weights = held.tile([P, M], BF16, name="weights")
+        bias = held.tile([P, BLOCKS], F32, name="bias")
+        pooled = held.tile([P, BLOCKS, V], F32, name="pooled")
+
+        nc.sync.dma_start(offsets[:], offs)
+        nc.scalar.dma_start(nodes[:], table)
+        nc.sync.dma_start(weights[:], w)
+        nc.scalar.dma_start(bias[:], b.rearrange("(a p) o -> p (a o)", p=P))
+
+        for a in range(BLOCKS):
+            product = psum.tile([P, N], F32, name=f"product{a}")
+            nc.tensor.matmul(
+                product[:],
+                weights[:, a * P : (a + 1) * P],
+                nodes[:].indirect(offsets[:]),
+                start=True,
+                stop=True,
+            )
+            nc.vector.tensor_reduce(
+                pooled[:, a, :],
+                product[:].rearrange("p (v t) -> p v t", t=GROUP),
+                axis=mybir.AxisListType.X,
+                op=mybir.AluOpType.max,
+            )
+            nc.vector.tensor_scalar_add(pooled[:, a, :], pooled[:, a, :], bias[:, a : a + 1])
+
+        nc.sync.dma_start(out.rearrange("(a p) v -> p a v", p=P), pooled[:])

@@ -46,5 +46,5 @@ def tile_gather_matmul_kernel(tc, table, w, b, offs, out):
                 op=mybir.AluOpType.max,
             )
             nc.vector.tensor_scalar_add(pooled[:, a, :], pooled[:, a, :], bias[:, a : a + 1])
-
-        nc.sync.dma_start(out.rearrange("(a p) v -> p a v", p=P), pooled[:])
+            store_queue = nc.sync if a % 2 == 0 else nc.scalar
+            store_queue.dma_start(out[a * P : (a + 1) * P, :], pooled[:, a, :])

@@ -9,6 +9,7 @@ N = 192
 GROUP = 4
 V = N // GROUP
 BLOCKS = M // P
+WARM_UPS = 4
 
 FLOPS = 2 * P * M * N
 
@@ -29,6 +30,12 @@ def tile_gather_matmul_kernel(tc, table, w, b, offs, out):
         nc.scalar.dma_start(nodes[:], table)
         nc.sync.dma_start(weights[:], w)
         nc.scalar.dma_start(bias[:], b.rearrange("(a p) o -> p (a o)", p=P))
+
+        zeros = held.tile([P, S], BF16, name="zeros")
+        unused = psum.tile([P, S], F32, name="unused")
+        nc.vector.memset(zeros[:], 0.0)
+        for i in range(WARM_UPS):
+            nc.tensor.matmul(unused[:], zeros[:, 0:P], zeros[:], start=True, stop=True)
 
         for a in range(BLOCKS):
             product = psum.tile([P, N], F32, name=f"product{a}")

@@ -9,10 +9,8 @@ N = 192
 GROUP = 4
 V = N // GROUP
 BLOCKS = M // P
-WARM_UPS = 4
 
 FLOPS = 2 * P * M * N
-
 
 def tile_gather_matmul_kernel(tc, table, w, b, offs, out):
     nc = tc.nc
@@ -30,12 +28,6 @@ def tile_gather_matmul_kernel(tc, table, w, b, offs, out):
         nc.scalar.dma_start(nodes[:], table)
         nc.sync.dma_start(weights[:], w)
         nc.scalar.dma_start(bias[:], b.rearrange("(a p) o -> p (a o)", p=P))
-
-        zeros = held.tile([P, S], BF16, name="zeros")
-        unused = psum.tile([P, S], F32, name="unused")
-        nc.vector.memset(zeros[:], 0.0)
-        for i in range(WARM_UPS):
-            nc.tensor.matmul(unused[:], zeros[:, 0:P], zeros[:], start=True, stop=True)
 
         for a in range(BLOCKS):
             product = psum.tile([P, N], F32, name=f"product{a}")

@@ -24,9 +24,9 @@ def tile_gather_matmul_kernel(tc, table, w, b, offs, out):
         bias = held.tile([P, BLOCKS], F32, name="bias")
         pooled = held.tile([P, BLOCKS, V], F32, name="pooled")
 
-        nc.sync.dma_start(offsets[:], offs)
         nc.scalar.dma_start(nodes[:], table)
         nc.sync.dma_start(weights[:], w)
+        nc.sync.dma_start(offsets[:], offs)
         nc.scalar.dma_start(bias[:], b.rearrange("(a p) o -> p (a o)", p=P))
 
         for a in range(BLOCKS):

@@ -30,20 +30,23 @@ def tile_gather_matmul_kernel(tc, table, w, b, offs, out):
         nc.scalar.dma_start(bias[:], b.rearrange("(a p) o -> p (a o)", p=P))
 
         for a in range(BLOCKS):
-            product = psum.tile([P, N], F32, name=f"product{a}")
-            nc.tensor.matmul(
-                product[:],
-                weights[:, a * P : (a + 1) * P],
-                nodes[:].indirect(offsets[:]),
-                start=True,
-                stop=True,
-            )
-            nc.vector.tensor_reduce(
-                pooled[:, a, :],
-                product[:].rearrange("p (v t) -> p v t", t=GROUP),
-                axis=mybir.AxisListType.X,
-                op=mybir.AluOpType.max,
-            )
-            nc.vector.tensor_scalar_add(pooled[:, a, :], pooled[:, a, :], bias[:, a : a + 1])
+            pieces = ((0, 2 * N // 3), (2 * N // 3, N)) if a == BLOCKS - 1 else ((0, N),)
+            for first, end in pieces:
+                product = psum.tile([P, end - first], F32, name=f"product{a}_{first}")
+                nc.tensor.matmul(
+                    product[:],
+                    weights[:, a * P : (a + 1) * P],
+                    nodes[:].indirect(offsets[:, first // 16 : end // 16]),
+                    start=True,
+                    stop=True,
+                )
+                here = pooled[:, a, first // GROUP : end // GROUP]
+                nc.vector.tensor_reduce(
+                    here,
+                    product[:].rearrange("p (v t) -> p v t", t=GROUP),
+                    axis=mybir.AxisListType.X,
+                    op=mybir.AluOpType.max,
+                )
+                nc.vector.tensor_scalar_add(here, here, bias[:, a : a + 1])
             store_queue = nc.sync if a % 2 == 0 else nc.scalar
             store_queue.dma_start(out[a * P : (a + 1) * P, :], pooled[:, a, :])

import concourse.mybir as mybir

BF16, F32, U16 = mybir.dt.bfloat16, mybir.dt.float32, mybir.dt.uint16

P = 128
S = 512
M = 512
N = 192
GROUP = 4
V = N // GROUP
BLOCKS = M // P

FLOPS = 2 * P * M * N

def tile_gather_matmul_kernel(tc, table, w, b, offs, out):
    nc = tc.nc
    with (
        tc.tile_pool(name="held", bufs=1) as held,
        tc.psum_pool(name="psum", bufs=1) as psum,
    ):
        offsets = held.tile([P, N // 16], U16, name="offsets")
        nodes = held.tile([P, S], BF16, name="nodes")
        weights = held.tile([P, M], BF16, name="weights")
        bias = held.tile([P, BLOCKS], F32, name="bias")
        pooled = held.tile([P, BLOCKS, V], F32, name="pooled")

        nc.scalar.dma_start(nodes[:], table)
        nc.sync.dma_start(weights[:], w)
        nc.sync.dma_start(offsets[:], offs)
        nc.scalar.dma_start(bias[:], b.rearrange("(a p) o -> p (a o)", p=P))

        for a in range(BLOCKS):
            pieces = ((0, 2 * N // 3), (2 * N // 3, N)) if a == BLOCKS - 1 else ((0, N),)
            for first, end in pieces:
                product = psum.tile([P, end - first], F32, name=f"product{a}_{first}")
                nc.tensor.matmul(
                    product[:],
                    weights[:, a * P : (a + 1) * P],
                    nodes[:].indirect(offsets[:, first // 16 : end // 16]),
                    start=True,
                    stop=True,
                )
                here = pooled[:, a, first // GROUP : end // GROUP]
                nc.vector.tensor_reduce(
                    here,
                    product[:].rearrange("p (v t) -> p v t", t=GROUP),
                    axis=mybir.AxisListType.X,
                    op=mybir.AluOpType.max,
                )
                nc.vector.tensor_scalar_add(here, here, bias[:, a : a + 1])
            store_queue = nc.sync if a % 2 == 0 else nc.scalar
            store_queue.dma_start(out[a * P : (a + 1) * P, :], pooled[:, a, :])
